import numpy as np
import ml_dtypes

BF16 = ml_dtypes.bfloat16


def bf(x):
    return np.asarray(x, np.float32).astype(BF16)


def f32(x):
    return np.asarray(x, np.float32)


def f64(x):
    return np.asarray(x).astype(np.float64)


def striped(idx):
    return np.tile(idx.reshape(-1, 16).T, (8, 1))


S, K, M, N, D, V = 2048, 256, 128, 512, 2, 256


def setup_inputs():
    return {"table": bf(np.random.standard_normal((K, S))), "w": bf(np.random.standard_normal((D, K, M)) / np.sqrt(D * K)), "r": f32(np.random.standard_normal((M, V))), "offs": striped(np.random.permutation(np.tile(np.arange(S), 2))[:N])}


def reference(table, w, r, offs):
    idx = offs[:16].T.reshape(-1)
    x = f64(table)[:, idx]
    y = sum(f64(w)[t].T @ x[:, t * V : (t + 1) * V] for t in range(D))
    return y + f64(r)

@@ -1,0 +1,50 @@
+import concourse.mybir as mybir
+
+BF16, F32, U16 = mybir.dt.bfloat16, mybir.dt.float32, mybir.dt.uint16
+
+P = 128
+NODES = 2048
+FEATURES = 256
+BLOCKS = FEATURES // P
+ENDS = 2
+EDGES = 256
+OUT_FEATURES = 128
+EDGE_COLS = EDGES // 16
+
+FLOPS = 2 * ENDS * FEATURES * OUT_FEATURES * EDGES
+
+
+def tile_gather_matmul_kernel(tc, table, w, r, offs, out):
+    nc = tc.nc
+    with (
+        tc.tile_pool(name="held", bufs=1) as held,
+        tc.psum_pool(name="psum", bufs=1) as psum,
+    ):
+        offsets = held.tile([P, ENDS * EDGE_COLS], U16, name="offsets")
+        nc.sync.dma_start(offsets[:], offs)
+
+        weights = held.tile([P, ENDS * BLOCKS, OUT_FEATURES], BF16, name="weights")
+        nc.scalar.dma_start(weights[:], w.rearrange("t (b p) m -> p (t b) m", p=P))
+
+        blocks = [held.tile([P, NODES], BF16, name="block%d" % b) for b in range(BLOCKS)]
+        nc.sync.dma_start(blocks[0][:], table[0:P, :])
+        nc.scalar.dma_start(blocks[1][:], table[P : 2 * P, :])
+
+        edge_features = held.tile([P, EDGES], F32, name="edge_features")
+        nc.gpsimd.dma_start(edge_features[:], r)
+
+        acc = psum.tile([P, EDGES], F32, name="acc")
+        for b in range(BLOCKS):
+            for t in range(ENDS):
+                picked = blocks[b][:].indirect(offsets[:, t * EDGE_COLS : (t + 1) * EDGE_COLS])
+                nc.tensor.matmul(
+                    acc[:],
+                    weights[:, t * BLOCKS + b, :],
+                    picked,
+                    start=(b == 0 and t == 0),
+                    stop=(b == BLOCKS - 1 and t == ENDS - 1),
+                )
+
+        result = held.tile([P, EDGES], F32, name="result")
+        nc.vector.tensor_tensor(result[:], acc[:], edge_features[:], mybir.AluOpType.add)
+        nc.sync.dma_start(out, result[:])

@@ -27,11 +27,11 @@ def tile_gather_matmul_kernel(tc, table, w, r, offs, out):
         nc.scalar.dma_start(weights[:], w.rearrange("t (b p) m -> p (t b) m", p=P))
 
         blocks = [held.tile([P, NODES], BF16, name="block%d" % b) for b in range(BLOCKS)]
-        nc.sync.dma_start(blocks[0][:], table[0:P, :])
-        nc.scalar.dma_start(blocks[1][:], table[P : 2 * P, :])
+        for b in range(BLOCKS):
+            nc.sync.dma_start(blocks[b][:], table[b * P : (b + 1) * P, :])
 
         edge_features = held.tile([P, EDGES], F32, name="edge_features")
-        nc.gpsimd.dma_start(edge_features[:], r)
+        nc.sync.dma_start(edge_features[:], r)
 
         acc = psum.tile([P, EDGES], F32, name="acc")
         for b in range(BLOCKS):

@@ -11,6 +11,9 @@ EDGES = 256
 OUT_FEATURES = 128
 EDGE_COLS = EDGES // 16
 
+WARM_COLS = 512
+WARM_MATMULS = 6
+
 FLOPS = 2 * ENDS * FEATURES * OUT_FEATURES * EDGES
 
 
@@ -23,15 +26,22 @@ def tile_gather_matmul_kernel(tc, table, w, r, offs, out):
         offsets = held.tile([P, ENDS * EDGE_COLS], U16, name="offsets")
         nc.sync.dma_start(offsets[:], offs)
 
-        weights = held.tile([P, ENDS * BLOCKS, OUT_FEATURES], BF16, name="weights")
-        nc.scalar.dma_start(weights[:], w.rearrange("t (b p) m -> p (t b) m", p=P))
+        weights = held.tile([P, ENDS, BLOCKS, OUT_FEATURES], BF16, name="weights")
+        nc.scalar.dma_start(weights[:], w.rearrange("t (p b) m -> p t b m", b=BLOCKS))
 
         blocks = [held.tile([P, NODES], BF16, name="block%d" % b) for b in range(BLOCKS)]
+        table_blocks = table.rearrange("(p b) s -> b p s", b=BLOCKS)
         for b in range(BLOCKS):
-            nc.sync.dma_start(blocks[b][:], table[b * P : (b + 1) * P, :])
+            nc.sync.dma_start(blocks[b][:], table_blocks[b])
 
         edge_features = held.tile([P, EDGES], F32, name="edge_features")
         nc.sync.dma_start(edge_features[:], r)
+
+        zeros = held.tile([P, WARM_COLS], BF16, name="zeros")
+        nc.vector.memset(zeros[:], 0.0)
+        unread = psum.tile([P, WARM_COLS], F32, name="unread")
+        for i in range(WARM_MATMULS):
+            nc.tensor.matmul(unread[:], zeros[:, 0:P], zeros[:], start=True, stop=True)
 
         acc = psum.tile([P, EDGES], F32, name="acc")
         for b in range(BLOCKS):
@@ -39,7 +49,7 @@ def tile_gather_matmul_kernel(tc, table, w, r, offs, out):
                 picked = blocks[b][:].indirect(offsets[:, t * EDGE_COLS : (t + 1) * EDGE_COLS])
                 nc.tensor.matmul(
                     acc[:],
-                    weights[:, t * BLOCKS + b, :],
+                    weights[:, t, b, :],
                     picked,
                     start=(b == 0 and t == 0),
                     stop=(b == BLOCKS - 1 and t == ENDS - 1),

@@ -27,7 +27,7 @@ def tile_gather_matmul_kernel(tc, table, w, r, offs, out):
         nc.sync.dma_start(offsets[:], offs)
 
         weights = held.tile([P, ENDS, BLOCKS, OUT_FEATURES], BF16, name="weights")
-        nc.scalar.dma_start(weights[:], w.rearrange("t (p b) m -> p t b m", b=BLOCKS))
+        nc.sync.dma_start(weights[:], w.rearrange("t (p b) m -> p t b m", b=BLOCKS))
 
         blocks = [held.tile([P, NODES], BF16, name="block%d" % b) for b in range(BLOCKS)]
         table_blocks = table.rearrange("(p b) s -> b p s", b=BLOCKS)

@@ -11,9 +11,6 @@ EDGES = 256
 OUT_FEATURES = 128
 EDGE_COLS = EDGES // 16
 
-WARM_COLS = 512
-WARM_MATMULS = 6
-
 FLOPS = 2 * ENDS * FEATURES * OUT_FEATURES * EDGES
 
 
@@ -36,12 +33,6 @@ def tile_gather_matmul_kernel(tc, table, w, r, offs, out):
 
         edge_features = held.tile([P, EDGES], F32, name="edge_features")
         nc.sync.dma_start(edge_features[:], r)
-
-        zeros = held.tile([P, WARM_COLS], BF16, name="zeros")
-        nc.vector.memset(zeros[:], 0.0)
-        unread = psum.tile([P, WARM_COLS], F32, name="unread")
-        for i in range(WARM_MATMULS):
-            nc.tensor.matmul(unread[:], zeros[:, 0:P], zeros[:], start=True, stop=True)
 
         acc = psum.tile([P, EDGES], F32, name="acc")
         for b in range(BLOCKS):

@@ -20,18 +20,16 @@ def tile_gather_matmul_kernel(tc, table, w, r, offs, out):
         tc.tile_pool(name="held", bufs=1) as held,
         tc.psum_pool(name="psum", bufs=1) as psum,
     ):
-        offsets = held.tile([P, ENDS * EDGE_COLS], U16, name="offsets")
-        nc.sync.dma_start(offsets[:], offs)
-
-        weights = held.tile([P, ENDS, BLOCKS, OUT_FEATURES], BF16, name="weights")
-        nc.sync.dma_start(weights[:], w.rearrange("t (p b) m -> p t b m", b=BLOCKS))
-
         blocks = [held.tile([P, NODES], BF16, name="block%d" % b) for b in range(BLOCKS)]
         table_blocks = table.rearrange("(p b) s -> b p s", b=BLOCKS)
-        for b in range(BLOCKS):
-            nc.sync.dma_start(blocks[b][:], table_blocks[b])
-
+        offsets = held.tile([P, ENDS * EDGE_COLS], U16, name="offsets")
+        weights = held.tile([P, ENDS, BLOCKS, OUT_FEATURES], BF16, name="weights")
         edge_features = held.tile([P, EDGES], F32, name="edge_features")
+
+        nc.sync.dma_start(blocks[0][:], table_blocks[0])
+        nc.sync.dma_start(offsets[:], offs)
+        nc.sync.dma_start(weights[:], w.rearrange("t (p b) m -> p t b m", b=BLOCKS))
+        nc.sync.dma_start(blocks[1][:], table_blocks[1])
         nc.sync.dma_start(edge_features[:], r)
 
         acc = psum.tile([P, EDGES], F32, name="acc")

@@ -27,8 +27,8 @@ def tile_gather_matmul_kernel(tc, table, w, r, offs, out):
         edge_features = held.tile([P, EDGES], F32, name="edge_features")
 
         nc.sync.dma_start(blocks[0][:], table_blocks[0])
-        nc.sync.dma_start(offsets[:], offs)
         nc.sync.dma_start(weights[:], w.rearrange("t (p b) m -> p t b m", b=BLOCKS))
+        nc.sync.dma_start(offsets[:], offs)
         nc.sync.dma_start(blocks[1][:], table_blocks[1])
         nc.sync.dma_start(edge_features[:], r)
 

import concourse.mybir as mybir

BF16, F32, U16 = mybir.dt.bfloat16, mybir.dt.float32, mybir.dt.uint16

P = 128
NODES = 2048
FEATURES = 256
BLOCKS = FEATURES // P
ENDS = 2
EDGES = 256
OUT_FEATURES = 128
EDGE_COLS = EDGES // 16

FLOPS = 2 * ENDS * FEATURES * OUT_FEATURES * EDGES


def tile_gather_matmul_kernel(tc, table, w, r, offs, out):
    nc = tc.nc
    with (
        tc.tile_pool(name="held", bufs=1) as held,
        tc.psum_pool(name="psum", bufs=1) as psum,
    ):
        blocks = [held.tile([P, NODES], BF16, name="block%d" % b) for b in range(BLOCKS)]
        table_blocks = table.rearrange("(p b) s -> b p s", b=BLOCKS)
        offsets = held.tile([P, ENDS * EDGE_COLS], U16, name="offsets")
        weights = held.tile([P, ENDS, BLOCKS, OUT_FEATURES], BF16, name="weights")
        edge_features = held.tile([P, EDGES], F32, name="edge_features")

        nc.sync.dma_start(blocks[0][:], table_blocks[0])
        nc.sync.dma_start(weights[:], w.rearrange("t (p b) m -> p t b m", b=BLOCKS))
        nc.sync.dma_start(offsets[:], offs)
        nc.sync.dma_start(blocks[1][:], table_blocks[1])
        nc.sync.dma_start(edge_features[:], r)

        acc = psum.tile([P, EDGES], F32, name="acc")
        for b in range(BLOCKS):
            for t in range(ENDS):
                picked = blocks[b][:].indirect(offsets[:, t * EDGE_COLS : (t + 1) * EDGE_COLS])
                nc.tensor.matmul(
                    acc[:],
                    weights[:, t, b, :],
                    picked,
                    start=(b == 0 and t == 0),
                    stop=(b == BLOCKS - 1 and t == ENDS - 1),
                )

        result = held.tile([P, EDGES], F32, name="result")
        nc.vector.tensor_tensor(result[:], acc[:], edge_features[:], mybir.AluOpType.add)
        nc.sync.dma_start(out, result[:])
